import numpy as np
import ml_dtypes


def mxq(x, axis, fmt="e4m3"):
    dtype, down = {"e4m3": (ml_dtypes.float8_e4m3fn, 7), "e5m2": (ml_dtypes.float8_e5m2, 14)}[fmt]
    v = np.moveaxis(np.asarray(x, np.float32).astype(ml_dtypes.bfloat16).astype(np.float64), axis, -1)
    blocks = v.reshape(v.shape[:-1] + (-1, 32))
    amax = np.abs(blocks).max(-1, keepdims=True)
    byte = np.maximum(np.where(amax > 0, np.frexp(amax)[1] - 1 + 127, 0) - down, 1)
    scale = np.exp2(byte - 127.0)
    codes = (blocks / scale).astype(np.float32).astype(dtype).astype(np.float64)
    return np.moveaxis((codes * scale).reshape(v.shape), -1, axis)


WIDE = False


def mx_kscale(k):
    if not WIDE:
        return np.ones(k)
    levels = np.array([10, -10, 5, -5, 0])
    if k % 512:
        return np.exp2(np.random.permutation(np.resize(levels, k // 32))).repeat(32)
    a = np.empty((k // 512, 16))
    for p in range(k // 512):
        a[p, :8] = np.random.permutation(np.resize(levels, 8))
        for g in range(8):
            far = levels[np.abs(levels - a[p, g]) >= 10]
            a[p, g + 8] = far[np.random.randint(len(far))]
    return np.exp2(a.ravel()).repeat(32)


def f64(x):
    return np.asarray(x).astype(np.float64)


def striped8(idx):
    return np.asarray(idx).reshape(8, -1, 16).transpose(0, 2, 1).reshape(128, -1).astype(np.uint16)


def unstriped8(offs):
    return offs.reshape(8, 16, -1).transpose(0, 2, 1).reshape(8, -1).astype(np.int64)


def pick8(x, idx, run):
    r = np.arange(len(x))
    return x[r[:, None], idx[r % (8 * run) // run]]


E2M1 = np.array([0.0, 0.5, 1.0, 1.5, 2.0, 3.0, 4.0, 6.0, -0.0, -0.5, -1.0, -1.5, -2.0, -3.0, -4.0, -6.0])


def pack_weight(w, fmt):
    k, n = w.shape
    w = f64(np.asarray(w, np.float32).astype(ml_dtypes.bfloat16)).reshape(k // 32, 32, n)
    amax = np.abs(w).max(1)
    if fmt == "e4m3":
        byte = np.frexp(amax)[1] - 1 + 127 - 7
    else:
        mant, ex = np.frexp(amax / 6.0)
        byte = np.where(mant > 0.5, ex, ex - 1) + 127
    byte = np.clip(np.where(amax > 0, byte, 1), 1, 254)
    scaled = (w * np.exp2(127.0 - byte)[:, None, :]).reshape(k, n).astype(np.float32)
    by_word = np.ascontiguousarray(scaled.reshape(k // 512, 128, 4, n).transpose(0, 1, 3, 2))
    if fmt == "e4m3":
        words = by_word.astype(ml_dtypes.float8_e4m3fn).view(np.uint8)
    else:
        c = by_word.astype(ml_dtypes.float4_e2m1fn).view(np.uint8) & 0xF
        words = (c[..., 0::2] | (c[..., 1::2] << 4)).reshape(k // 512, 128, 2 * n)
    return np.ascontiguousarray(words), np.ascontiguousarray(byte.astype(np.uint8).reshape(k // 512, 16, n))


def unpack_weight(words, scales, fmt):
    g, _, n = scales.shape
    words = np.ascontiguousarray(words).reshape(g, 128, n, -1)
    if fmt == "e4m3":
        vals = words.view(ml_dtypes.float8_e4m3fn).astype(np.float64)
    else:
        nib = np.empty((g, 128, n, 4), np.uint8)
        nib[..., 0::2] = words & 0xF
        nib[..., 1::2] = words >> 4
        vals = E2M1[nib]
    vals = vals * np.repeat(np.exp2(scales.astype(np.float64) - 127.0), 8, axis=1)[..., None]
    return vals.transpose(0, 1, 3, 2).reshape(g * 512, n)


D, T, I, Q, E = 512, 1024, 512, 512, 256


def setup_inputs():
    n = np.random.standard_normal
    idx = np.stack([np.random.permutation(T)[:I] for _ in range(8)])
    idx2 = np.stack([np.random.permutation(T)[:I] for _ in range(8)])
    idx3 = np.stack([np.random.permutation(T)[:I] for _ in range(8)])
    idx4 = np.stack([np.random.permutation(T)[:I] for _ in range(8)])
    idx5 = np.stack([np.random.permutation(T)[:I] for _ in range(8)])
    fd = mx_kscale(D)
    fq = mx_kscale(Q)
    cachep = pack_weight(n((D, T)) / fd[:, None], "e2m1")
    mixp = pack_weight(n((Q, E)) * 1.0 / np.sqrt(Q) / fq[:, None], "e4m3")
    return {
        "query": (n((D, Q)) * 1.0 / np.sqrt(D) * fd[:, None]).astype(np.float32),
        "cache_words": cachep[0],
        "cache_scales": cachep[1],
        "rowf": (np.random.uniform(0.5, 2.0, (Q, 1)) * fq[:, None]).astype(np.float32),
        "mix_words": mixp[0],
        "mix_scales": mixp[1],
        "offs": striped8(idx),
        "offs2": striped8(idx2),
        "offs3": striped8(idx3),
        "offs4": striped8(idx4),
        "offs5": striped8(idx5),
    }


def reference(query, cache_words, cache_scales, rowf, mix_words, mix_scales, offs, offs2, offs3, offs4, offs5):
    idx = unstriped8(offs)
    idx2 = unstriped8(offs2)
    idx3 = unstriped8(offs3)
    idx4 = unstriped8(offs4)
    idx5 = unstriped8(offs5)
    cacheu = unpack_weight(cache_words, cache_scales, "e2m1")
    mixu = unpack_weight(mix_words, mix_scales, "e4m3")
    queryq = mxq(f64(query), 0, "e4m3")
    a = queryq.T @ cacheu
    f1 = np.zeros((Q, T))
    f1[np.arange(Q)[:, None], idx2[np.arange(Q) % 512 // 64]] = pick8(a, idx, 64)
    c1 = a - f1
    f2 = np.zeros((Q, T))
    f2[np.arange(Q)[:, None], idx[np.arange(Q) % 512 // 64]] = pick8(c1, idx3, 64)
    c2 = np.maximum(c1, f2)
    g = pick8(c2, idx4, 64) + pick8(c1, idx5, 64)
    gw = g * f64(rowf)
    gwq = mxq(gw, 0, "e4m3")
    y = mixu.T @ gwq
    return y

@@ -1,0 +1,236 @@
+from contextlib import ExitStack
+
+import concourse.mybir as mybir
+
+F32 = mybir.dt.float32
+BF16 = mybir.dt.bfloat16
+I32 = mybir.dt.int32
+U16 = mybir.dt.uint16
+U8 = mybir.dt.uint8
+E4M3X4 = mybir.dt.float8_e4m3fn_x4
+E2M1X4 = mybir.dt.float4_e2m1fn_x4
+ALU = mybir.AluOpType
+COPY = mybir.ActivationFunctionType.Copy
+
+D, T, I, Q, E = 512, 1024, 512, 512, 256
+P = 128
+PACK = 4
+BANK = 512
+HALF = I // 2
+LIST_COLS = I // 16
+
+FLOPS = 2 * D * Q * T + 2 * Q * E * I
+
+
+def tile_attend_backpair_one_mixed_kernel(
+    tc, query, cache_words, cache_scales, rowf, mix_words, mix_scales, offs, offs2, offs3, offs4, offs5, out
+):
+    nc = tc.nc
+    with ExitStack() as ctx:
+        sb = ctx.enter_context(tc.tile_pool(name="sb", bufs=1))
+        ps = ctx.enter_context(tc.psum_pool(name="ps", bufs=1))
+
+        idx = sb.tile([P, LIST_COLS], U16, name="idx")
+        idx2 = sb.tile([P, LIST_COLS], U16, name="idx2")
+        idx3 = sb.tile([P, LIST_COLS], U16, name="idx3")
+        idx4 = sb.tile([P, LIST_COLS], U16, name="idx4")
+        idx5 = sb.tile([P, LIST_COLS], U16, name="idx5")
+
+        cache_plane = sb.tile([P, T], U8, name="cache_plane", align_bytes=64)
+        mix_plane = sb.tile([P, E], U8, name="mix_plane", align_bytes=64)
+        cache_codes = sb.tile([P, 2 * T], U8, name="cache_codes", align_bytes=64)
+        mix_codes = sb.tile([P, E], I32, name="mix_codes", align_bytes=64)
+        factors = sb.tile([P, PACK], F32, name="factors")
+        q_raw = [sb.tile([P, PACK, Q // 2], F32, name=f"q_raw{c}") for c in range(2)]
+        f1 = [sb.tile([P, T], F32, name=f"f1_{b}") for b in range(2)]
+        f2 = [sb.tile([P, T], F32, name=f"f2_{b}") for b in range(2)]
+
+        nc.vector.memset(cache_plane[:].bitcast(I32), 0)
+        q_rows = query.rearrange("(p j) q -> p j q", j=PACK)
+        for c in range(2):
+            nc.sync.dma_start(out=q_raw[c][:], in_=q_rows[:, :, c * (Q // 2) : (c + 1) * (Q // 2)])
+        nc.sync.dma_start(out=cache_codes[:].bitcast(I32), in_=cache_words[0].bitcast(I32))
+        for quad in range(4):
+            nc.scalar.dma_start(
+                out=cache_plane[32 * quad : 32 * quad + 4, :].bitcast(I32),
+                in_=cache_scales[0, 4 * quad : 4 * quad + 4, :].bitcast(I32),
+            )
+        nc.sync.dma_start(idx[:], offs)
+        nc.sync.dma_start(idx2[:], offs2)
+        nc.sync.dma_start(idx3[:], offs3)
+        nc.sync.dma_start(idx5[:], offs5)
+        nc.sync.dma_start(idx4[:], offs4)
+
+        for window in (f1[0], f1[1], f2[0], f2[1]):
+            nc.vector.memset(window[:], 0.0)
+        nc.vector.memset(mix_plane[:].bitcast(I32), 0)
+        nc.sync.dma_start(out=factors[:], in_=rowf.rearrange("(p r) o -> p (r o)", r=PACK))
+        nc.sync.dma_start(out=mix_codes[:], in_=mix_words[0].rearrange("p e t -> p (e t)").bitcast(I32))
+        for quad in range(4):
+            nc.sync.dma_start(
+                out=mix_plane[32 * quad : 32 * quad + 4, :].bitcast(I32),
+                in_=mix_scales[0, 4 * quad : 4 * quad + 4, :].bitcast(I32),
+            )
+
+        q_bf = sb.tile([P, PACK, P, PACK], BF16, name="q_bf", align_bytes=64)
+        q_codes = sb.tile([P, Q], I32, name="q_codes", align_bytes=64)
+        q_plane = sb.tile([P, Q], U8, name="q_plane", align_bytes=64)
+
+        def deal(c, r0, r1):
+            nc.vector.tensor_copy(
+                out=q_bf[:, r0:r1, c * (P // 2) : (c + 1) * (P // 2), :].rearrange("p r s j -> p s j r"),
+                in_=q_raw[c][:].rearrange("p j (s r) -> p s j r", r=PACK)[:, :, :, r0:r1],
+            )
+
+        deal(0, 0, PACK)
+        for r0, r1 in ((0, 1), (1, PACK)):
+            deal(1, r0, r1)
+            nc.vector.quantize_mx(
+                out=q_codes[:, r0 * P : r1 * P].bitcast(E4M3X4),
+                scales=q_plane[:, r0 * P : r1 * P],
+                in_=q_bf[:, r0:r1, :, :].rearrange("p r s j -> p (r s j)"),
+            )
+
+        score_banks = [[ps.tile([P, BANK], F32, name=f"bank{2 * r + u}") for u in range(2)] for r in range(PACK)]
+        for r in range(PACK):
+            for u in range(2):
+                nc.tensor.matmul_mx(
+                    out=score_banks[r][u][:],
+                    lhsT=q_codes[:, r * P : (r + 1) * P].bitcast(E4M3X4),
+                    lhsT_scale=q_plane[:, r * P : (r + 1) * P],
+                    rhs=cache_codes[:, 2 * u * BANK : 2 * (u + 1) * BANK].bitcast(E2M1X4),
+                    rhs_scale=cache_plane[:, u * BANK : (u + 1) * BANK],
+                    start=True,
+                    stop=True,
+                )
+
+        a = [sb.tile([P, T], F32, name=f"a{r}") for r in range(PACK)]
+        c1 = [sb.tile([P, T], F32, name=f"c1_{r}") for r in range(PACK)]
+        c2 = [sb.tile([P, T], F32, name=f"c2_{r}") for r in range(PACK)]
+        a_picked = [sb.tile([P, I], F32, name=f"a_picked{r}") for r in range(PACK)]
+        c1_by3 = [sb.tile([P, I], F32, name=f"c1_by3_{r}") for r in range(PACK)]
+        c1_by5 = [sb.tile([P, I], F32, name=f"c1_by5_{r}") for r in range(PACK - 1)] + [c1_by3[PACK - 1]]
+        g = [sb.tile([P, I], F32, name=f"g{r}") for r in range(PACK)]
+        pairs = sb.tile([P, 2, I, 2], BF16, name="pairs")
+        gw = sb.tile([P, I, PACK], BF16, name="gw", align_bytes=64)
+        gw_codes = sb.tile([P, I], I32, name="gw_codes", align_bytes=64)
+        gw_plane = sb.tile([P, I], U8, name="gw_plane", align_bytes=64)
+
+        def slots(h):
+            return slice(h * HALF, (h + 1) * HALF)
+
+        def entries(h):
+            return slice(h * LIST_COLS // 2, (h + 1) * LIST_COLS // 2)
+
+        def empty_bank(r, u, on_scalar=False):
+            dst = a[r][:, u * BANK : (u + 1) * BANK]
+            if on_scalar:
+                nc.scalar.copy(out=dst, in_=score_banks[r][u][:])
+            else:
+                nc.vector.tensor_copy(out=dst, in_=score_banks[r][u][:])
+
+        def pick_a(r):
+            nc.vector.tensor_copy(a_picked[r][:], a[r][:].indirect(idx[:]))
+
+        def put_f1(r):
+            nc.scalar.activation(f1[r % 2][:].indirect(idx2[:]), a_picked[r][:], COPY)
+
+        def make_c1(r):
+            nc.vector.tensor_tensor(c1[r][:], a[r][:], f1[r % 2][:], ALU.subtract)
+
+        def pick_by3(r):
+            nc.vector.tensor_copy(c1_by3[r][:], c1[r][:].indirect(idx3[:]))
+
+        def put_f2(r):
+            nc.scalar.activation(f2[r % 2][:].indirect(idx[:]), c1_by3[r][:], COPY)
+
+        def pick_by5(r):
+            nc.vector.tensor_copy(c1_by5[r][:], c1[r][:].indirect(idx5[:]))
+
+        def make_c2(r):
+            nc.vector.tensor_tensor(c2[r][:], c1[r][:], f2[r % 2][:], ALU.max)
+
+        def make_g(r):
+            nc.vector.tensor_tensor(g[r][:], c2[r][:].indirect(idx4[:]), c1_by5[r][:], ALU.add)
+
+        def weigh_on_vector(r):
+            nc.vector.tensor_scalar(pairs[:, r // 2, :, r % 2], g[r][:], factors[:, r : r + 1], None, ALU.mult)
+
+        def weigh_on_scalar(r, cols):
+            nc.scalar.activation(pairs[:, r // 2, cols, r % 2], g[r][:, cols], COPY, scale=factors[:, r : r + 1])
+
+        empty_bank(0, 0, on_scalar=True)
+        empty_bank(0, 1)
+        nc.vector.tensor_copy(a_picked[0][:, slots(0)], a[0][:].indirect(idx[:, entries(0)]))
+        nc.scalar.activation(a_picked[0][:, slots(1)], a[0][:].indirect(idx[:, entries(1)]), COPY)
+        put_f1(0)
+        empty_bank(1, 0)
+        empty_bank(1, 1)
+        pick_a(1)
+        put_f1(1)
+        empty_bank(2, 0)
+        empty_bank(2, 1)
+        make_c1(0)
+        pick_by3(0)
+        put_f2(0)
+        pick_a(2)
+        empty_bank(3, 1, on_scalar=True)
+        put_f1(2)
+        make_c1(1)
+        pick_by3(1)
+        put_f2(1)
+        empty_bank(3, 0)
+        pick_a(3)
+        put_f1(3)
+        pick_by5(0)
+        make_c2(0)
+        make_c1(2)
+        pick_by3(2)
+        put_f2(2)
+        make_g(0)
+        pick_by5(1)
+        weigh_on_vector(0)
+        make_c2(1)
+        make_c1(3)
+        make_g(1)
+        pick_by3(3)
+        put_f2(3)
+        weigh_on_vector(1)
+        pick_by5(2)
+        make_c2(2)
+        nc.scalar.activation(c1_by5[3][:], c1[3][:].indirect(idx5[:]), COPY)
+        make_g(2)
+        weigh_on_scalar(2, slice(0, I))
+        make_c2(3)
+        for h in range(2):
+            nc.vector.tensor_tensor(
+                g[3][:, slots(h)], c2[3][:].indirect(idx4[:, entries(h)]), c1_by5[3][:, slots(h)], ALU.add
+            )
+            weigh_on_scalar(3, slots(h))
+
+        pair_words = pairs[:].rearrange("p u i e -> p u (i e)").bitcast(F32)
+        gw_words = gw[:].bitcast(F32)
+        for h in range(2):
+            nc.vector.tensor_copy(out=gw_words[:, slots(h), :], in_=pair_words[:, :, slots(h)].rearrange("p u i -> p i u"))
+            nc.vector.quantize_mx(
+                out=gw_codes[:, slots(h)].bitcast(E4M3X4),
+                scales=gw_plane[:, slots(h)],
+                in_=gw[:, slots(h), :].rearrange("p i r -> p (i r)"),
+            )
+            for m in range(E // P):
+                acc = ps.tile([P, BANK], F32, name=f"acc{h}{m}", tag=f"bank{2 * h + m}")
+                nc.tensor.matmul_mx(
+                    out=acc[:, :HALF],
+                    lhsT=mix_codes[:, m * P : (m + 1) * P].bitcast(E4M3X4),
+                    lhsT_scale=mix_plane[:, m * P : (m + 1) * P],
+                    rhs=gw_codes[:, slots(h)].bitcast(E4M3X4),
+                    rhs_scale=gw_plane[:, slots(h)],
+                    start=True,
+                    stop=True,
+                )
+                result = sb.tile([P, HALF], F32, name=f"result{h}{m}")
+                if h == 1 and m == 1:
+                    nc.vector.tensor_copy(out=result[:], in_=acc[:, :HALF])
+                else:
+                    nc.scalar.copy(out=result[:], in_=acc[:, :HALF])
+                nc.sync.dma_start(out=out[m * P : (m + 1) * P, slots(h)], in_=result[:])

@@ -76,42 +76,42 @@ def tile_attend_backpair_one_mixed_kernel(
         q_codes = sb.tile([P, Q], I32, name="q_codes", align_bytes=64)
         q_plane = sb.tile([P, Q], U8, name="q_plane", align_bytes=64)
 
-        def deal(c, r0, r1):
-            nc.vector.tensor_copy(
+        def deal(copy, c, r0, r1):
+            copy(
                 out=q_bf[:, r0:r1, c * (P // 2) : (c + 1) * (P // 2), :].rearrange("p r s j -> p s j r"),
                 in_=q_raw[c][:].rearrange("p j (s r) -> p s j r", r=PACK)[:, :, :, r0:r1],
             )
 
-        deal(0, 0, PACK)
-        for r0, r1 in ((0, 1), (1, PACK)):
-            deal(1, r0, r1)
+        def quantise_rows(r0, r1):
             nc.vector.quantize_mx(
                 out=q_codes[:, r0 * P : r1 * P].bitcast(E4M3X4),
                 scales=q_plane[:, r0 * P : r1 * P],
                 in_=q_bf[:, r0:r1, :, :].rearrange("p r s j -> p (r s j)"),
             )
 
-        score_banks = [[ps.tile([P, BANK], F32, name=f"bank{2 * r + u}") for u in range(2)] for r in range(PACK)]
-        for r in range(PACK):
-            for u in range(2):
-                nc.tensor.matmul_mx(
-                    out=score_banks[r][u][:],
-                    lhsT=q_codes[:, r * P : (r + 1) * P].bitcast(E4M3X4),
-                    lhsT_scale=q_plane[:, r * P : (r + 1) * P],
-                    rhs=cache_codes[:, 2 * u * BANK : 2 * (u + 1) * BANK].bitcast(E2M1X4),
-                    rhs_scale=cache_plane[:, u * BANK : (u + 1) * BANK],
-                    start=True,
-                    stop=True,
-                )
+        deal(nc.vector.tensor_copy, 0, 0, 2)
+        deal(nc.vector.tensor_copy, 1, 0, 1)
+        quantise_rows(0, 1)
+        deal(nc.vector.tensor_copy, 1, 1, 2)
+        for c in range(2):
+            deal(nc.scalar.copy, c, 2, PACK)
 
-        a = [sb.tile([P, T], F32, name=f"a{r}") for r in range(PACK)]
-        c1 = [sb.tile([P, T], F32, name=f"c1_{r}") for r in range(PACK)]
-        c2 = [sb.tile([P, T], F32, name=f"c2_{r}") for r in range(PACK)]
-        a_picked = [sb.tile([P, I], F32, name=f"a_picked{r}") for r in range(PACK)]
-        c1_by3 = [sb.tile([P, I], F32, name=f"c1_by3_{r}") for r in range(PACK)]
-        c1_by5 = [sb.tile([P, I], F32, name=f"c1_by5_{r}") for r in range(PACK - 1)] + [c1_by3[PACK - 1]]
-        g = [sb.tile([P, I], F32, name=f"g{r}") for r in range(PACK)]
-        pairs = sb.tile([P, 2, I, 2], BF16, name="pairs")
+        def wide(name, tag):
+            return sb.tile([P, T], F32, name=name, tag=tag)
+
+        def narrow(name, tag):
+            return sb.tile([P, I], F32, name=name, tag=tag)
+
+        a = [wide(f"a{r}", f"a{r}") for r in range(PACK)]
+        c1 = [wide(f"c1_{r}", f"c1_{r}") for r in range(PACK)]
+        a_picked = [narrow(f"a_picked{r}", f"a_picked{r}") for r in range(PACK)]
+        shared = wide("shared", "shared")
+        c1_by3 = [narrow(f"c1_by3_{r}", f"c1_by3_{r}")[:] for r in range(PACK - 1)] + [shared[:, I:]]
+        c1_by5 = [shared[:, HALF : HALF + I], narrow("c1_by5_1", "c1_by5_1")[:], shared[:, :I], shared[:, I:]]
+        g = [narrow(f"g{r}", f"g{r}") for r in range(PACK)]
+        c2_tags = ["a2", "a2", "g0", "g1"]
+        c2 = {}
+        c2_by4 = sb.tile([P, HALF], F32, name="c2_by4")
         gw = sb.tile([P, I, PACK], BF16, name="gw", align_bytes=64)
         gw_codes = sb.tile([P, I], I32, name="gw_codes", align_bytes=64)
         gw_plane = sb.tile([P, I], U8, name="gw_plane", align_bytes=64)
@@ -122,12 +122,22 @@ def tile_attend_backpair_one_mixed_kernel(
         def entries(h):
             return slice(h * LIST_COLS // 2, (h + 1) * LIST_COLS // 2)
 
-        def empty_bank(r, u, on_scalar=False):
+        def score(r, u, on_scalar=False):
+            bank = ps.tile([P, BANK], F32, name=f"score{r}{u}", tag=f"bank{2 * max(r - 1, 0) + u}")
+            nc.tensor.matmul_mx(
+                out=bank[:],
+                lhsT=q_codes[:, r * P : (r + 1) * P].bitcast(E4M3X4),
+                lhsT_scale=q_plane[:, r * P : (r + 1) * P],
+                rhs=cache_codes[:, 2 * u * BANK : 2 * (u + 1) * BANK].bitcast(E2M1X4),
+                rhs_scale=cache_plane[:, u * BANK : (u + 1) * BANK],
+                start=True,
+                stop=True,
+            )
             dst = a[r][:, u * BANK : (u + 1) * BANK]
             if on_scalar:
-                nc.scalar.copy(out=dst, in_=score_banks[r][u][:])
+                nc.scalar.copy(out=dst, in_=bank[:])
             else:
-                nc.vector.tensor_copy(out=dst, in_=score_banks[r][u][:])
+                nc.vector.tensor_copy(out=dst, in_=bank[:])
 
         def pick_a(r):
             nc.vector.tensor_copy(a_picked[r][:], a[r][:].indirect(idx[:]))
@@ -136,82 +146,87 @@ def tile_attend_backpair_one_mixed_kernel(
             nc.scalar.activation(f1[r % 2][:].indirect(idx2[:]), a_picked[r][:], COPY)
 
         def make_c1(r):
-            nc.vector.tensor_tensor(c1[r][:], a[r][:], f1[r % 2][:], ALU.subtract)
+            nc.gpsimd.tensor_tensor(c1[r][:], a[r][:], f1[r % 2][:], ALU.subtract)
 
         def pick_by3(r):
-            nc.vector.tensor_copy(c1_by3[r][:], c1[r][:].indirect(idx3[:]))
+            nc.vector.tensor_copy(c1_by3[r], c1[r][:].indirect(idx3[:]))
 
         def put_f2(r):
-            nc.scalar.activation(f2[r % 2][:].indirect(idx[:]), c1_by3[r][:], COPY)
+            nc.scalar.activation(f2[r % 2][:].indirect(idx[:]), c1_by3[r], COPY)
 
         def pick_by5(r):
-            nc.vector.tensor_copy(c1_by5[r][:], c1[r][:].indirect(idx5[:]))
+            nc.vector.tensor_copy(c1_by5[r], c1[r][:].indirect(idx5[:]))
 
         def make_c2(r):
+            c2.update({r: wide(f"c2_{r}", c2_tags[r])})
             nc.vector.tensor_tensor(c2[r][:], c1[r][:], f2[r % 2][:], ALU.max)
 
         def make_g(r):
-            nc.vector.tensor_tensor(g[r][:], c2[r][:].indirect(idx4[:]), c1_by5[r][:], ALU.add)
+            nc.vector.tensor_tensor(g[r][:], c2[r][:].indirect(idx4[:]), c1_by5[r], ALU.add)
 
-        def weigh_on_vector(r):
-            nc.vector.tensor_scalar(pairs[:, r // 2, :, r % 2], g[r][:], factors[:, r : r + 1], None, ALU.mult)
+        def weigh(r, cols):
+            nc.vector.tensor_scalar(pairs[:, r // 2, cols, r % 2], g[r][:, cols], factors[:, r : r + 1], None, ALU.mult)
 
-        def weigh_on_scalar(r, cols):
-            nc.scalar.activation(pairs[:, r // 2, cols, r % 2], g[r][:, cols], COPY, scale=factors[:, r : r + 1])
-
-        empty_bank(0, 0, on_scalar=True)
-        empty_bank(0, 1)
+        every = slice(0, I)
+        score(0, 0)
+        score(0, 1, on_scalar=True)
+        quantise_rows(1, 2)
+        quantise_rows(2, PACK)
         nc.vector.tensor_copy(a_picked[0][:, slots(0)], a[0][:].indirect(idx[:, entries(0)]))
         nc.scalar.activation(a_picked[0][:, slots(1)], a[0][:].indirect(idx[:, entries(1)]), COPY)
         put_f1(0)
-        empty_bank(1, 0)
-        empty_bank(1, 1)
+        score(1, 0)
+        score(1, 1)
+        score(2, 0)
         pick_a(1)
         put_f1(1)
-        empty_bank(2, 0)
-        empty_bank(2, 1)
+        score(2, 1)
         make_c1(0)
+        score(3, 0)
+        pick_a(2)
+        put_f1(2)
+        score(3, 1)
         pick_by3(0)
         put_f2(0)
-        pick_a(2)
-        empty_bank(3, 1, on_scalar=True)
-        put_f1(2)
         make_c1(1)
-        pick_by3(1)
-        put_f2(1)
-        empty_bank(3, 0)
         pick_a(3)
         put_f1(3)
         pick_by5(0)
-        make_c2(0)
         make_c1(2)
-        pick_by3(2)
-        put_f2(2)
-        make_g(0)
+        pick_by3(1)
+        put_f2(1)
         pick_by5(1)
-        weigh_on_vector(0)
-        make_c2(1)
+        pick_by3(2)
+        make_c2(0)
+        put_f2(2)
         make_c1(3)
-        make_g(1)
-        pick_by3(3)
-        put_f2(3)
-        weigh_on_vector(1)
+        make_g(0)
         pick_by5(2)
+        pick_by3(3)
+        make_c2(1)
+        put_f2(3)
+        pairs = sb.tile([P, 2, I, 2], BF16, name="pairs", tag="c1_1")
+        weigh(0, every)
+        make_g(1)
         make_c2(2)
-        nc.scalar.activation(c1_by5[3][:], c1[3][:].indirect(idx5[:]), COPY)
+        weigh(1, every)
         make_g(2)
-        weigh_on_scalar(2, slice(0, I))
+        nc.scalar.activation(c1_by5[3], c1[3][:].indirect(idx5[:]), COPY)
         make_c2(3)
+        weigh(2, every)
+        nc.scalar.activation(c2_by4[:], c2[3][:].indirect(idx4[:, entries(1)]), COPY)
+        nc.vector.tensor_tensor(
+            g[3][:, slots(0)], c2[3][:].indirect(idx4[:, entries(0)]), c1_by5[3][:, slots(0)], ALU.add
+        )
+        nc.vector.tensor_tensor(g[3][:, slots(1)], c2_by4[:], c1_by5[3][:, slots(1)], ALU.add)
         for h in range(2):
-            nc.vector.tensor_tensor(
-                g[3][:, slots(h)], c2[3][:].indirect(idx4[:, entries(h)]), c1_by5[3][:, slots(h)], ALU.add
-            )
-            weigh_on_scalar(3, slots(h))
+            weigh(3, slots(h))
 
         pair_words = pairs[:].rearrange("p u i e -> p u (i e)").bitcast(F32)
         gw_words = gw[:].bitcast(F32)
         for h in range(2):
             nc.vector.tensor_copy(out=gw_words[:, slots(h), :], in_=pair_words[:, :, slots(h)].rearrange("p u i -> p i u"))
+        for h in range(2):
             nc.vector.quantize_mx(
                 out=gw_codes[:, slots(h)].bitcast(E4M3X4),
                 scales=gw_plane[:, slots(h)],

@@ -41,14 +41,13 @@ def tile_attend_backpair_one_mixed_kernel(
         cache_codes = sb.tile([P, 2 * T], U8, name="cache_codes", align_bytes=64)
         mix_codes = sb.tile([P, E], I32, name="mix_codes", align_bytes=64)
         factors = sb.tile([P, PACK], F32, name="factors")
-        q_raw = [sb.tile([P, PACK, Q // 2], F32, name=f"q_raw{c}") for c in range(2)]
+        q_raw = [sb.tile([P, 2, Q], F32, name=f"q_raw{c}") for c in range(2)]
         f1 = [sb.tile([P, T], F32, name=f"f1_{b}") for b in range(2)]
         f2 = [sb.tile([P, T], F32, name=f"f2_{b}") for b in range(2)]
 
-        nc.vector.memset(cache_plane[:].bitcast(I32), 0)
         q_rows = query.rearrange("(p j) q -> p j q", j=PACK)
         for c in range(2):
-            nc.sync.dma_start(out=q_raw[c][:], in_=q_rows[:, :, c * (Q // 2) : (c + 1) * (Q // 2)])
+            nc.sync.dma_start(out=q_raw[c][:], in_=q_rows[:, 2 * c : 2 * c + 2, :])
         nc.sync.dma_start(out=cache_codes[:].bitcast(I32), in_=cache_words[0].bitcast(I32))
         for quad in range(4):
             nc.scalar.dma_start(
@@ -63,7 +62,6 @@ def tile_attend_backpair_one_mixed_kernel(
 
         for window in (f1[0], f1[1], f2[0], f2[1]):
             nc.vector.memset(window[:], 0.0)
-        nc.vector.memset(mix_plane[:].bitcast(I32), 0)
         nc.sync.dma_start(out=factors[:], in_=rowf.rearrange("(p r) o -> p (r o)", r=PACK))
         nc.sync.dma_start(out=mix_codes[:], in_=mix_words[0].rearrange("p e t -> p (e t)").bitcast(I32))
         for quad in range(4):
@@ -78,7 +76,7 @@ def tile_attend_backpair_one_mixed_kernel(
 
         def deal(copy, c, r0, r1):
             copy(
-                out=q_bf[:, r0:r1, c * (P // 2) : (c + 1) * (P // 2), :].rearrange("p r s j -> p s j r"),
+                out=q_bf[:, r0:r1, :, 2 * c : 2 * c + 2].rearrange("p r s j -> p s j r"),
                 in_=q_raw[c][:].rearrange("p j (s r) -> p s j r", r=PACK)[:, :, :, r0:r1],
             )
 
@@ -89,12 +87,12 @@ def tile_attend_backpair_one_mixed_kernel(
                 in_=q_bf[:, r0:r1, :, :].rearrange("p r s j -> p (r s j)"),
             )
 
-        deal(nc.vector.tensor_copy, 0, 0, 2)
+        deal(nc.vector.tensor_copy, 0, 0, 3)
         deal(nc.vector.tensor_copy, 1, 0, 1)
         quantise_rows(0, 1)
         deal(nc.vector.tensor_copy, 1, 1, 2)
-        for c in range(2):
-            deal(nc.scalar.copy, c, 2, PACK)
+        deal(nc.scalar.copy, 0, 3, PACK)
+        deal(nc.scalar.copy, 1, 2, PACK)
 
         def wide(name, tag):
             return sb.tile([P, T], F32, name=name, tag=tag)

@@ -101,13 +101,13 @@ def tile_attend_backpair_one_mixed_kernel(
             return sb.tile([P, I], F32, name=name, tag=tag)
 
         a = [wide(f"a{r}", f"a{r}") for r in range(PACK)]
-        c1 = [wide(f"c1_{r}", f"c1_{r}") for r in range(PACK)]
+        c1 = [wide(f"c1_{r}", f"c1_{r}") for r in range(PACK - 1)]
         a_picked = [narrow(f"a_picked{r}", f"a_picked{r}") for r in range(PACK)]
-        shared = wide("shared", "shared")
-        c1_by3 = [narrow(f"c1_by3_{r}", f"c1_by3_{r}")[:] for r in range(PACK - 1)] + [shared[:, I:]]
-        c1_by5 = [shared[:, HALF : HALF + I], narrow("c1_by5_1", "c1_by5_1")[:], shared[:, :I], shared[:, I:]]
+        c1_by3 = [narrow(f"c1_by3_{r}", f"c1_by3_{r}")[:] for r in range(PACK)]
+        c1_by5 = [narrow(f"c1_by5_{r}", f"c1_by5_{r}")[:] for r in range(PACK - 1)] + [c1_by3[PACK - 1]]
+        first_by4 = narrow("first_by4", "first_by4")
         g = [narrow(f"g{r}", f"g{r}") for r in range(PACK)]
-        c2_tags = ["a2", "a2", "g0", "g1"]
+        c2_tags = ["a2", "first_by4", "g0", "g1"]
         c2 = {}
         c2_by4 = sb.tile([P, HALF], F32, name="c2_by4")
         gw = sb.tile([P, I, PACK], BF16, name="gw", align_bytes=64)
@@ -136,6 +136,7 @@ def tile_attend_backpair_one_mixed_kernel(
                 nc.scalar.copy(out=dst, in_=bank[:])
             else:
                 nc.vector.tensor_copy(out=dst, in_=bank[:])
+            return bank
 
         def pick_a(r):
             nc.vector.tensor_copy(a_picked[r][:], a[r][:].indirect(idx[:]))
@@ -183,7 +184,7 @@ def tile_attend_backpair_one_mixed_kernel(
         score(3, 0)
         pick_a(2)
         put_f1(2)
-        score(3, 1)
+        last_bank = score(3, 1)
         pick_by3(0)
         put_f2(0)
         make_c1(1)
@@ -197,9 +198,12 @@ def tile_attend_backpair_one_mixed_kernel(
         pick_by3(2)
         make_c2(0)
         put_f2(2)
-        make_c1(3)
-        make_g(0)
         pick_by5(2)
+        nc.vector.tensor_copy(first_by4[:], c2[0][:].indirect(idx4[:]))
+        c1.append(wide("c1_3", "c1_0"))
+        nc.gpsimd.tensor_tensor(c1[3][:, :BANK], a[3][:, :BANK], f1[1][:, :BANK], ALU.subtract)
+        nc.vector.tensor_tensor(c1[3][:, BANK:], last_bank[:], f1[1][:, BANK:], ALU.subtract)
+        nc.vector.tensor_tensor(g[0][:], first_by4[:], c1_by5[0], ALU.add)
         pick_by3(3)
         make_c2(1)
         put_f2(3)

from contextlib import ExitStack

import concourse.mybir as mybir

F32 = mybir.dt.float32
BF16 = mybir.dt.bfloat16
I32 = mybir.dt.int32
U16 = mybir.dt.uint16
U8 = mybir.dt.uint8
E4M3X4 = mybir.dt.float8_e4m3fn_x4
E2M1X4 = mybir.dt.float4_e2m1fn_x4
ALU = mybir.AluOpType
COPY = mybir.ActivationFunctionType.Copy

D, T, I, Q, E = 512, 1024, 512, 512, 256
P = 128
PACK = 4
BANK = 512
HALF = I // 2
LIST_COLS = I // 16

FLOPS = 2 * D * Q * T + 2 * Q * E * I


def tile_attend_backpair_one_mixed_kernel(
    tc, query, cache_words, cache_scales, rowf, mix_words, mix_scales, offs, offs2, offs3, offs4, offs5, out
):
    nc = tc.nc
    with ExitStack() as ctx:
        sb = ctx.enter_context(tc.tile_pool(name="sb", bufs=1))
        ps = ctx.enter_context(tc.psum_pool(name="ps", bufs=1))

        idx = sb.tile([P, LIST_COLS], U16, name="idx")
        idx2 = sb.tile([P, LIST_COLS], U16, name="idx2")
        idx3 = sb.tile([P, LIST_COLS], U16, name="idx3")
        idx4 = sb.tile([P, LIST_COLS], U16, name="idx4")
        idx5 = sb.tile([P, LIST_COLS], U16, name="idx5")

        cache_plane = sb.tile([P, T], U8, name="cache_plane", align_bytes=64)
        mix_plane = sb.tile([P, E], U8, name="mix_plane", align_bytes=64)
        cache_codes = sb.tile([P, 2 * T], U8, name="cache_codes", align_bytes=64)
        mix_codes = sb.tile([P, E], I32, name="mix_codes", align_bytes=64)
        factors = sb.tile([P, PACK], F32, name="factors")
        q_raw = [sb.tile([P, 2, Q], F32, name=f"q_raw{c}") for c in range(2)]
        f1 = [sb.tile([P, T], F32, name=f"f1_{b}") for b in range(2)]
        f2 = [sb.tile([P, T], F32, name=f"f2_{b}") for b in range(2)]

        q_rows = query.rearrange("(p j) q -> p j q", j=PACK)
        for c in range(2):
            nc.sync.dma_start(out=q_raw[c][:], in_=q_rows[:, 2 * c : 2 * c + 2, :])
        nc.sync.dma_start(out=cache_codes[:].bitcast(I32), in_=cache_words[0].bitcast(I32))
        for quad in range(4):
            nc.scalar.dma_start(
                out=cache_plane[32 * quad : 32 * quad + 4, :].bitcast(I32),
                in_=cache_scales[0, 4 * quad : 4 * quad + 4, :].bitcast(I32),
            )
        nc.sync.dma_start(idx[:], offs)
        nc.sync.dma_start(idx2[:], offs2)
        nc.sync.dma_start(idx3[:], offs3)
        nc.sync.dma_start(idx5[:], offs5)
        nc.sync.dma_start(idx4[:], offs4)

        for window in (f1[0], f1[1], f2[0], f2[1]):
            nc.vector.memset(window[:], 0.0)
        nc.sync.dma_start(out=factors[:], in_=rowf.rearrange("(p r) o -> p (r o)", r=PACK))
        nc.sync.dma_start(out=mix_codes[:], in_=mix_words[0].rearrange("p e t -> p (e t)").bitcast(I32))
        for quad in range(4):
            nc.sync.dma_start(
                out=mix_plane[32 * quad : 32 * quad + 4, :].bitcast(I32),
                in_=mix_scales[0, 4 * quad : 4 * quad + 4, :].bitcast(I32),
            )

        q_bf = sb.tile([P, PACK, P, PACK], BF16, name="q_bf", align_bytes=64)
        q_codes = sb.tile([P, Q], I32, name="q_codes", align_bytes=64)
        q_plane = sb.tile([P, Q], U8, name="q_plane", align_bytes=64)

        def deal(copy, c, r0, r1):
            copy(
                out=q_bf[:, r0:r1, :, 2 * c : 2 * c + 2].rearrange("p r s j -> p s j r"),
                in_=q_raw[c][:].rearrange("p j (s r) -> p s j r", r=PACK)[:, :, :, r0:r1],
            )

        def quantise_rows(r0, r1):
            nc.vector.quantize_mx(
                out=q_codes[:, r0 * P : r1 * P].bitcast(E4M3X4),
                scales=q_plane[:, r0 * P : r1 * P],
                in_=q_bf[:, r0:r1, :, :].rearrange("p r s j -> p (r s j)"),
            )

        deal(nc.vector.tensor_copy, 0, 0, 3)
        deal(nc.vector.tensor_copy, 1, 0, 1)
        quantise_rows(0, 1)
        deal(nc.vector.tensor_copy, 1, 1, 2)
        deal(nc.scalar.copy, 0, 3, PACK)
        deal(nc.scalar.copy, 1, 2, PACK)

        def wide(name, tag):
            return sb.tile([P, T], F32, name=name, tag=tag)

        def narrow(name, tag):
            return sb.tile([P, I], F32, name=name, tag=tag)

        a = [wide(f"a{r}", f"a{r}") for r in range(PACK)]
        c1 = [wide(f"c1_{r}", f"c1_{r}") for r in range(PACK - 1)]
        a_picked = [narrow(f"a_picked{r}", f"a_picked{r}") for r in range(PACK)]
        c1_by3 = [narrow(f"c1_by3_{r}", f"c1_by3_{r}")[:] for r in range(PACK)]
        c1_by5 = [narrow(f"c1_by5_{r}", f"c1_by5_{r}")[:] for r in range(PACK - 1)] + [c1_by3[PACK - 1]]
        first_by4 = narrow("first_by4", "first_by4")
        g = [narrow(f"g{r}", f"g{r}") for r in range(PACK)]
        c2_tags = ["a2", "first_by4", "g0", "g1"]
        c2 = {}
        c2_by4 = sb.tile([P, HALF], F32, name="c2_by4")
        gw = sb.tile([P, I, PACK], BF16, name="gw", align_bytes=64)
        gw_codes = sb.tile([P, I], I32, name="gw_codes", align_bytes=64)
        gw_plane = sb.tile([P, I], U8, name="gw_plane", align_bytes=64)

        def slots(h):
            return slice(h * HALF, (h + 1) * HALF)

        def entries(h):
            return slice(h * LIST_COLS // 2, (h + 1) * LIST_COLS // 2)

        def score(r, u, on_scalar=False):
            bank = ps.tile([P, BANK], F32, name=f"score{r}{u}", tag=f"bank{2 * max(r - 1, 0) + u}")
            nc.tensor.matmul_mx(
                out=bank[:],
                lhsT=q_codes[:, r * P : (r + 1) * P].bitcast(E4M3X4),
                lhsT_scale=q_plane[:, r * P : (r + 1) * P],
                rhs=cache_codes[:, 2 * u * BANK : 2 * (u + 1) * BANK].bitcast(E2M1X4),
                rhs_scale=cache_plane[:, u * BANK : (u + 1) * BANK],
                start=True,
                stop=True,
            )
            dst = a[r][:, u * BANK : (u + 1) * BANK]
            if on_scalar:
                nc.scalar.copy(out=dst, in_=bank[:])
            else:
                nc.vector.tensor_copy(out=dst, in_=bank[:])
            return bank

        def pick_a(r):
            nc.vector.tensor_copy(a_picked[r][:], a[r][:].indirect(idx[:]))

        def put_f1(r):
            nc.scalar.activation(f1[r % 2][:].indirect(idx2[:]), a_picked[r][:], COPY)

        def make_c1(r):
            nc.gpsimd.tensor_tensor(c1[r][:], a[r][:], f1[r % 2][:], ALU.subtract)

        def pick_by3(r):
            nc.vector.tensor_copy(c1_by3[r], c1[r][:].indirect(idx3[:]))

        def put_f2(r):
            nc.scalar.activation(f2[r % 2][:].indirect(idx[:]), c1_by3[r], COPY)

        def pick_by5(r):
            nc.vector.tensor_copy(c1_by5[r], c1[r][:].indirect(idx5[:]))

        def make_c2(r):
            c2.update({r: wide(f"c2_{r}", c2_tags[r])})
            nc.vector.tensor_tensor(c2[r][:], c1[r][:], f2[r % 2][:], ALU.max)

        def make_g(r):
            nc.vector.tensor_tensor(g[r][:], c2[r][:].indirect(idx4[:]), c1_by5[r], ALU.add)

        def weigh(r, cols):
            nc.vector.tensor_scalar(pairs[:, r // 2, cols, r % 2], g[r][:, cols], factors[:, r : r + 1], None, ALU.mult)

        every = slice(0, I)
        score(0, 0)
        score(0, 1, on_scalar=True)
        quantise_rows(1, 2)
        quantise_rows(2, PACK)
        nc.vector.tensor_copy(a_picked[0][:, slots(0)], a[0][:].indirect(idx[:, entries(0)]))
        nc.scalar.activation(a_picked[0][:, slots(1)], a[0][:].indirect(idx[:, entries(1)]), COPY)
        put_f1(0)
        score(1, 0)
        score(1, 1)
        score(2, 0)
        pick_a(1)
        put_f1(1)
        score(2, 1)
        make_c1(0)
        score(3, 0)
        pick_a(2)
        put_f1(2)
        last_bank = score(3, 1)
        pick_by3(0)
        put_f2(0)
        make_c1(1)
        pick_a(3)
        put_f1(3)
        pick_by5(0)
        make_c1(2)
        pick_by3(1)
        put_f2(1)
        pick_by5(1)
        pick_by3(2)
        make_c2(0)
        put_f2(2)
        pick_by5(2)
        nc.vector.tensor_copy(first_by4[:], c2[0][:].indirect(idx4[:]))
        c1.append(wide("c1_3", "c1_0"))
        nc.gpsimd.tensor_tensor(c1[3][:, :BANK], a[3][:, :BANK], f1[1][:, :BANK], ALU.subtract)
        nc.vector.tensor_tensor(c1[3][:, BANK:], last_bank[:], f1[1][:, BANK:], ALU.subtract)
        nc.vector.tensor_tensor(g[0][:], first_by4[:], c1_by5[0], ALU.add)
        pick_by3(3)
        make_c2(1)
        put_f2(3)
        pairs = sb.tile([P, 2, I, 2], BF16, name="pairs", tag="c1_1")
        weigh(0, every)
        make_g(1)
        make_c2(2)
        weigh(1, every)
        make_g(2)
        nc.scalar.activation(c1_by5[3], c1[3][:].indirect(idx5[:]), COPY)
        make_c2(3)
        weigh(2, every)
        nc.scalar.activation(c2_by4[:], c2[3][:].indirect(idx4[:, entries(1)]), COPY)
        nc.vector.tensor_tensor(
            g[3][:, slots(0)], c2[3][:].indirect(idx4[:, entries(0)]), c1_by5[3][:, slots(0)], ALU.add
        )
        nc.vector.tensor_tensor(g[3][:, slots(1)], c2_by4[:], c1_by5[3][:, slots(1)], ALU.add)
        for h in range(2):
            weigh(3, slots(h))

        pair_words = pairs[:].rearrange("p u i e -> p u (i e)").bitcast(F32)
        gw_words = gw[:].bitcast(F32)
        for h in range(2):
            nc.vector.tensor_copy(out=gw_words[:, slots(h), :], in_=pair_words[:, :, slots(h)].rearrange("p u i -> p i u"))
        for h in range(2):
            nc.vector.quantize_mx(
                out=gw_codes[:, slots(h)].bitcast(E4M3X4),
                scales=gw_plane[:, slots(h)],
                in_=gw[:, slots(h), :].rearrange("p i r -> p (i r)"),
            )
            for m in range(E // P):
                acc = ps.tile([P, BANK], F32, name=f"acc{h}{m}", tag=f"bank{2 * h + m}")
                nc.tensor.matmul_mx(
                    out=acc[:, :HALF],
                    lhsT=mix_codes[:, m * P : (m + 1) * P].bitcast(E4M3X4),
                    lhsT_scale=mix_plane[:, m * P : (m + 1) * P],
                    rhs=gw_codes[:, slots(h)].bitcast(E4M3X4),
                    rhs_scale=gw_plane[:, slots(h)],
                    start=True,
                    stop=True,
                )
                result = sb.tile([P, HALF], F32, name=f"result{h}{m}")
                if h == 1 and m == 1:
                    nc.vector.tensor_copy(out=result[:], in_=acc[:, :HALF])
                else:
                    nc.scalar.copy(out=result[:], in_=acc[:, :HALF])
                nc.sync.dma_start(out=out[m * P : (m + 1) * P, slots(h)], in_=result[:])
